import numpy as np, ml_dtypes
CORES = [33,34,161,162,289,290,417,418]
N = 8
import mx_ref
NC = 256
SEQ = [0,0,0,1,1,1,1,2]
WID = [128,138,232,256,216,202,134,174]
BF = ml_dtypes.bfloat16
def setup_inputs(rng):
    def f(*shape):
        return mx_ref.flush((rng.standard_normal(shape, dtype=np.float32) * np.exp2(rng.integers(-2, 3, shape[:-1] + (1,)))).astype(BF))
    return {"w": f(N, 128, 512), "x": f(N, 128, 4 * NC)}
def setup_inputs_blocks(rng):
    d = setup_inputs(rng)
    for k in ("w", "x"): d[k] = mx_ref.spread(d[k], rng, 4)
    return d
def setup_inputs_wide(rng):
    d = setup_inputs(rng)
    for k in ("w", "x"): d[k] = mx_ref.flush((d[k].astype(np.float32) * np.exp2(rng.integers(-10, 11, (N, 1, 1))).astype(np.float32)).astype(BF))
    return d
def reference(w, x):
    y = np.full((N, 128, 808), np.nan, np.float32)
    for r in range(N):
        qw = mx_ref.quantize(w[r]); a = 0
        for j in range(N):
            if SEQ[j] == SEQ[r]:
                y[r][:, a:a + WID[j]] = mx_ref.matmul(qw, mx_ref.quantize(x[j][:, :4 * WID[j]])); a += WID[j]
    return {"y": y}

@@ -1,0 +1,140 @@
+from concourse.bass import DstId, RemoteDMATransfer
+from concourse.mybir import dt, ActivationFunctionType
+
+LAND = 832
+MOST = 4
+
+SCRATCH = {
+    "xb": ("sbuf", [128, 1024], "bfloat16"),
+    "wb": ("sbuf", [128, 512], "bfloat16"),
+    "wq": ("sbuf", [128, 128], "float8_e4m3fn_x4"),
+    "wp": ("sbuf", [128, 128], "uint8"),
+    "xq": ("sbuf", [128, LAND], "float8_e4m3fn_x4"),
+    "xp": ("sbuf", [128, LAND], "uint8"),
+    "ps": ("psum", [128, 512 * MOST], "float32"),
+    "yb": ("sbuf", [128, 808], "float32"),
+}
+SEMAPHORES = (["ldx", "ldw", "qx", "qw", "sent", "st"]
+              + [k + str(i) for k in ("c", "p", "m", "v") for i in range(MOST)])
+
+CODES, PLANE = "c", "p"
+
+
+def _engines(mask):
+    return [e for e in range(mask.bit_length()) if (mask >> e) & 1]
+
+
+def _plan(cores, seq, topo):
+    n = len(cores)
+    place = [(topo.host(c), topo.chip(c)) for c in cores]
+    leave, stay, onward = [[] for _ in cores], [[] for _ in cores], [[] for _ in cores]
+    for j in range(n):
+        mem = [d for d in range(n) if seq[d] == seq[j]]
+        near = [d for d in mem if d != j and place[d] == place[j]]
+        chips = {}
+        for d in mem:
+            if place[d] != place[j]:
+                chips.setdefault(place[d], []).append(d)
+        reach = [grp for grp in chips.values() if all(topo.may_write(cores[j], cores[d]) for d in grp)]
+        shut = [d for grp in chips.values() if grp not in reach for d in grp]
+        door = None
+        if shut:
+            door = max([grp for grp in reach if all(topo.may_write(cores[m], cores[d]) for m in grp for d in shut)],
+                       key=len)
+        for k, kind in enumerate((CODES, PLANE)):
+            gates = [grp[(mem.index(j) + k) % len(grp)] for grp in reach]
+            if gates:
+                leave[j].append((j, kind, gates))
+            if near:
+                stay[j].append((j, kind, near))
+            for grp, gate in zip(reach, gates):
+                more = [d for d in grp if d != gate] + (shut if grp is door else [])
+                if more:
+                    onward[gate].append((j, kind, more))
+    calls, arrive = [], {}
+    for r in range(n):
+        away = set()
+        for d in range(n):
+            if place[d] != place[r] and topo.may_write(cores[r], cores[d]):
+                away |= set(_engines(topo.mask(cores[r], cores[d])))
+        mine = []
+        todo = leave[r] + stay[r] + sorted(onward[r], key=lambda c: c[1] != CODES)
+        for pos, (j, kind, dsts) in enumerate(todo):
+            far = [d for d in dsts if place[d] != place[r]]
+            home = [d for d in dsts if place[d] == place[r]]
+            legs = [(d, _engines(topo.mask(cores[r], cores[d]))[i::len(far)]) for i, d in enumerate(far)]
+            legs += [(d, [e for e in _engines(topo.mask(cores[r], cores[d])) if e not in away][i::len(home)])
+                     for i, d in enumerate(home)]
+            for d, eng in legs:
+                arrive[(d, j, kind)] = (len(eng), (1 if j == r else 2, pos))
+            mine.append((j, kind, legs))
+        calls.append(mine)
+    return calls, arrive
+
+
+def rank_program(g, core, T, topo):
+    r = T.rank_of(core)
+    if r is None:
+        return
+    cores, seq, wid, S = T.cores, T.tables["SEQ"], T.tables["WID"], T.sem
+    calls, arrive = _plan(cores, seq, topo)
+    mem = [j for j in range(len(cores)) if seq[j] == seq[r]]
+    slot = {j: i for i, j in enumerate(mem)}
+    land, out, a, b = {}, {}, 0, 0
+    for j in mem:
+        land[j], out[j] = a, b
+        a, b = a + (wid[j] + 15) // 16 * 16, b + wid[j]
+
+    def codes(j):
+        return T.xq[:, land[j]:land[j] + wid[j]]
+
+    def plane(j):
+        return T.xp[:, land[j]:land[j] + wid[j]]
+
+    g.sync.dma_start(T.xb[:, :4 * wid[r]], T.x[:, :4 * wid[r]]).then_inc(S.ldx, 16)
+    g.sync.dma_start(T.wb[:], T.w[:]).then_inc(S.ldw, 16)
+    g.vector.wait_ge(S.ldx, 16)
+    g.vector.quantize_mx(codes(r), plane(r), T.xb[:, :4 * wid[r]]).then_inc(S.qx, 1)
+    g.vector.wait_ge(S.ldw, 16)
+    g.vector.quantize_mx(T.wq[:], T.wp[:], T.wb[:]).then_inc(S.qw, 1)
+
+    sent = 0
+    for j, kind, legs in calls[r]:
+        if j == r:
+            g.wait_ge(S.qx, 1)
+        else:
+            g.wait_ge(S[kind + str(slot[j])], arrive[(r, j, kind)][0])
+        view = codes(j).bitcast(dt.uint8) if kind == CODES else plane(j)
+        transfers = []
+        for d, eng in legs:
+            rid, pid = topo.addr(cores[d], core)
+            transfers.append(RemoteDMATransfer(dst_ids=[DstId(rid=rid, pnc=pid)], dma_engine_mask=sum(1 << e for e in eng),
+                                               remote_sem=S[kind + str(slot[j])], src=view, dst=view))
+            sent += len(eng)
+        g.remote_dma_fused(transfers, local_sem=S.sent)
+
+    order = [r] + sorted((j for j in mem if j != r), key=lambda j: max(arrive[(r, j, k)][1] for k in (CODES, PLANE)))
+    g.tensor.wait_ge(S.qw, 1)
+    g.tensor.wait_ge(S.qx, 1)
+    for i, j in enumerate(order):
+        if j != r:
+            for kind in (CODES, PLANE):
+                g.tensor.wait_ge(S[kind + str(slot[j])], arrive[(r, j, kind)][0])
+        acc = T.ps[:, 512 * i:512 * i + wid[j]]
+        blk = T.yb[:, out[j]:out[j] + wid[j]]
+        done, copied = S["m" + str(i)], S["v" + str(i)]
+        g.tensor.matmul_mx(acc, T.wq[:], T.wp[:], codes(j), plane(j), True, True).then_inc(done, 1)
+        if (len(order) - 1 - i) % 2 == 0:
+            g.vector.wait_ge(done, 1)
+            g.vector.tensor_copy(blk, acc).then_inc(copied, 1)
+            q = g.sync
+        else:
+            g.scalar.wait_ge(done, 1)
+            g.scalar.activation(blk, acc, ActivationFunctionType.Copy).then_inc(copied, 1)
+            q = g.scalar
+        q.wait_ge(copied, 1)
+        q.dma_start(T.y[:, out[j]:out[j] + wid[j]], blk).then_inc(S.st, 16)
+
+    if sent:
+        g.wait_ge(S.sent, sent)
+    g.wait_ge(S.st, 16 * len(order))

@@ -3,6 +3,8 @@ from concourse.mybir import dt, ActivationFunctionType
 
 LAND = 832
 MOST = 4
+WORLD = 512
+PIECE = 128
 
 SCRATCH = {
     "xb": ("sbuf", [128, 1024], "bfloat16"),
@@ -11,79 +13,138 @@ SCRATCH = {
     "wp": ("sbuf", [128, 128], "uint8"),
     "xq": ("sbuf", [128, LAND], "float8_e4m3fn_x4"),
     "xp": ("sbuf", [128, LAND], "uint8"),
+    "xr": ("sbuf", [128, 128], "float8_e4m3fn_x4"),
     "ps": ("psum", [128, 512 * MOST], "float32"),
     "yb": ("sbuf", [128, 808], "float32"),
 }
 SEMAPHORES = (["ldx", "ldw", "qx", "qw", "sent", "st"]
-              + [k + str(i) for k in ("c", "p", "m", "v") for i in range(MOST)])
+              + [k + str(i) for k in ("c", "d", "p", "m", "v") for i in range(MOST)])
 
-CODES, PLANE = "c", "p"
+CODES, REST, PLANE = "c", "d", "p"
+_KEEP = {}
 
 
 def _engines(mask):
     return [e for e in range(mask.bit_length()) if (mask >> e) & 1]
 
 
-def _plan(cores, seq, topo):
+def _plan(cores, seq, wid, topo):
     n = len(cores)
-    place = [(topo.host(c), topo.chip(c)) for c in cores]
-    leave, stay, onward = [[] for _ in cores], [[] for _ in cores], [[] for _ in cores]
-    for j in range(n):
-        mem = [d for d in range(n) if seq[d] == seq[j]]
-        near = [d for d in mem if d != j and place[d] == place[j]]
+
+    def place(c):
+        return (topo.host(c), topo.chip(c))
+
+    def away(c):
+        out = set()
+        for d in cores:
+            if place(d) != place(c) and topo.may_write(c, d):
+                out |= set(_engines(topo.mask(c, d)))
+        return out
+
+    def full(c, d):
+        return _engines(topo.mask(c, d))
+
+    def home(c, d):
+        return [e for e in full(c, d) if e not in away(c)]
+
+    calls, cut, late, park = {}, set(), set(), set()
+
+    def call(c, j, kind, legs):
+        calls.setdefault(c, []).append((j, kind, legs))
+
+    for s in sorted(set(seq)):
+        mem = [j for j in range(n) if seq[j] == s]
         chips = {}
-        for d in mem:
-            if place[d] != place[j]:
-                chips.setdefault(place[d], []).append(d)
-        reach = [grp for grp in chips.values() if all(topo.may_write(cores[j], cores[d]) for d in grp)]
-        shut = [d for grp in chips.values() if grp not in reach for d in grp]
-        door = None
-        if shut:
-            door = max([grp for grp in reach if all(topo.may_write(cores[m], cores[d]) for m in grp for d in shut)],
-                       key=len)
-        for k, kind in enumerate((CODES, PLANE)):
-            gates = [grp[(mem.index(j) + k) % len(grp)] for grp in reach]
-            if gates:
-                leave[j].append((j, kind, gates))
-            if near:
-                stay[j].append((j, kind, near))
-            for grp, gate in zip(reach, gates):
-                more = [d for d in grp if d != gate] + (shut if grp is door else [])
-                if more:
-                    onward[gate].append((j, kind, more))
-    calls, arrive = [], {}
-    for r in range(n):
-        away = set()
-        for d in range(n):
-            if place[d] != place[r] and topo.may_write(cores[r], cores[d]):
-                away |= set(_engines(topo.mask(cores[r], cores[d])))
-        mine = []
-        todo = leave[r] + stay[r] + sorted(onward[r], key=lambda c: c[1] != CODES)
-        for pos, (j, kind, dsts) in enumerate(todo):
-            far = [d for d in dsts if place[d] != place[r]]
-            home = [d for d in dsts if place[d] == place[r]]
-            legs = [(d, _engines(topo.mask(cores[r], cores[d]))[i::len(far)]) for i, d in enumerate(far)]
-            legs += [(d, [e for e in _engines(topo.mask(cores[r], cores[d])) if e not in away][i::len(home)])
-                     for i, d in enumerate(home)]
+        for j in mem:
+            chips.setdefault(place(cores[j]), []).append(j)
+        if all(topo.may_write(cores[a], cores[b]) for a in mem for b in mem if a != b):
+            leave, stay, onward = {j: [] for j in mem}, {j: [] for j in mem}, {j: [] for j in mem}
+            for j in mem:
+                near = [d for d in chips[place(cores[j])] if d != j]
+                reach = [grp for pl, grp in chips.items() if pl != place(cores[j])]
+                for k, kind in enumerate((CODES, PLANE)):
+                    gates = [grp[(mem.index(j) + k) % len(grp)] for grp in reach]
+                    if gates:
+                        leave[j].append((j, kind, gates))
+                    if near:
+                        stay[j].append((j, kind, near))
+                    for grp, gate in zip(reach, gates):
+                        more = [d for d in grp if d != gate]
+                        if more:
+                            onward[gate].append((j, kind, more))
+                            late.add(j)
+            for r in mem:
+                c = cores[r]
+                for j, kind, dsts in leave[r]:
+                    call(c, j, kind, [(cores[d], full(c, cores[d])[i::len(dsts)]) for i, d in enumerate(dsts)])
+                for j, kind, dsts in stay[r] + sorted(onward[r], key=lambda q: q[1] != CODES):
+                    call(c, j, kind, [(cores[d], home(c, cores[d])[i::len(dsts)]) for i, d in enumerate(dsts)])
+            continue
+        mid = max((grp for grp in chips.values()
+                   if all(topo.may_write(cores[a], cores[b]) and topo.may_write(cores[b], cores[a])
+                          for a in grp for b in mem if a != b)), key=len)
+        outer = [j for j in mem if j not in mid]
+        idle = sorted((c for c in range(WORLD) if place(c) == place(cores[mid[0]]) and c not in cores),
+                      key=lambda c: (topo.die(c) == topo.die(cores[mid[0]]), c))
+        carrier = {o: idle[i] for i, o in enumerate(outer)}
+        serves = {}
+        for o in outer:
+            for d in outer:
+                if d != o and not topo.may_write(cores[o], cores[d]):
+                    serves[d] = carrier[o]
+        for j in mid:
+            c = cores[j]
+            near = [d for d in mid if d != j]
+            round_ = [d for d in outer if d in serves and topo.same_plane(c, cores[d])]
+            straight = [d for d in outer if d not in round_]
+            call(c, j, CODES, [(cores[d], full(c, cores[d])[i::len(outer)]) for i, d in enumerate(outer)])
+            for d in round_:
+                call(c, j, PLANE, [(serves[d], home(c, serves[d]))])
+                call(serves[d], j, PLANE, [(cores[d], full(serves[d], cores[d]))])
+            if straight:
+                call(c, j, PLANE, [(cores[d], full(c, cores[d])[i::len(straight)]) for i, d in enumerate(straight)])
+            for kind in (CODES, PLANE):
+                call(c, j, kind, [(cores[d], home(c, cores[d])[i::len(near)]) for i, d in enumerate(near)])
+        for j in outer:
+            c, h = cores[j], carrier[j]
+            shut = [d for d in outer if d != j]
+            late.add(j)
+            beside = [b for b in cores if b != c and place(b) == place(c) and topo.may_write(b, h)
+                      and topo.rack(topo.host(c)) != topo.rack(topo.host(h))]
+            if wid[j] == 2 * PIECE and beside:
+                cut.add(j)
+                park.add((beside[0], j))
+                call(c, j, REST, [(beside[0], home(c, beside[0]))])
+                call(beside[0], j, REST, [(h, full(beside[0], h))])
+            for kind in (CODES, PLANE):
+                call(c, j, kind, [(h, full(c, h))])
+            for kind in (CODES, PLANE, REST) if j in cut else (CODES, PLANE):
+                call(h, j, kind, [(cores[d], full(h, cores[d])[i::len(shut)]) for i, d in enumerate(shut)]
+                     + [(cores[d], home(h, cores[d])[i::len(mid)]) for i, d in enumerate(mid)])
+
+    adds = {}
+    for c, todo in calls.items():
+        for j, kind, legs in todo:
             for d, eng in legs:
-                arrive[(d, j, kind)] = (len(eng), (1 if j == r else 2, pos))
-            mine.append((j, kind, legs))
-        calls.append(mine)
-    return calls, arrive
+                adds[(d, j, kind)] = len(eng)
+    return calls, adds, cut, late, park
 
 
 def rank_program(g, core, T, topo):
-    r = T.rank_of(core)
-    if r is None:
-        return
     cores, seq, wid, S = T.cores, T.tables["SEQ"], T.tables["WID"], T.sem
-    calls, arrive = _plan(cores, seq, topo)
-    mem = [j for j in range(len(cores)) if seq[j] == seq[r]]
-    slot = {j: i for i, j in enumerate(mem)}
-    land, out, a, b = {}, {}, 0, 0
-    for j in mem:
-        land[j], out[j] = a, b
-        a, b = a + (wid[j] + 15) // 16 * 16, b + wid[j]
+    if "plan" not in _KEEP:
+        _KEEP["plan"] = _plan(cores, seq, wid, topo)
+    calls, adds, cut, late, park = _KEEP["plan"]
+    r = T.rank_of(core)
+    if r is None and core not in calls:
+        return
+    n = len(cores)
+    slot, land, out = {}, {}, {}
+    for s in set(seq):
+        a = b = 0
+        for i, j in enumerate(j for j in range(n) if seq[j] == s):
+            slot[j], land[j], out[j] = i, a, b
+            a, b = a + (wid[j] + 15) // 16 * 16, b + wid[j]
 
     def codes(j):
         return T.xq[:, land[j]:land[j] + wid[j]]
@@ -91,35 +152,51 @@ def rank_program(g, core, T, topo):
     def plane(j):
         return T.xp[:, land[j]:land[j] + wid[j]]
 
-    g.sync.dma_start(T.xb[:, :4 * wid[r]], T.x[:, :4 * wid[r]]).then_inc(S.ldx, 16)
-    g.sync.dma_start(T.wb[:], T.w[:]).then_inc(S.ldw, 16)
-    g.vector.wait_ge(S.ldx, 16)
-    g.vector.quantize_mx(codes(r), plane(r), T.xb[:, :4 * wid[r]]).then_inc(S.qx, 1)
-    g.vector.wait_ge(S.ldw, 16)
-    g.vector.quantize_mx(T.wq[:], T.wp[:], T.wb[:]).then_inc(S.qw, 1)
+    def view(c, j, kind):
+        if kind == PLANE:
+            return plane(j)
+        if (c, j) in park:
+            return T.xr[:, :wid[j] - PIECE].bitcast(dt.uint8)
+        a, b = land[j], land[j] + wid[j]
+        if j in cut:
+            a, b = (a, a + PIECE) if kind == CODES else (a + PIECE, b)
+        return T.xq[:, a:b].bitcast(dt.uint8)
+
+    if r is not None:
+        g.sync.dma_start(T.xb[:, :4 * wid[r]], T.x[:, :4 * wid[r]]).then_inc(S.ldx, 16)
+        g.sync.dma_start(T.wb[:], T.w[:]).then_inc(S.ldw, 16)
+        g.vector.wait_ge(S.ldx, 16)
+        g.vector.quantize_mx(codes(r), plane(r), T.xb[:, :4 * wid[r]]).then_inc(S.qx, 1)
+        g.vector.wait_ge(S.ldw, 16)
+        g.vector.quantize_mx(T.wq[:], T.wp[:], T.wb[:]).then_inc(S.qw, 1)
 
     sent = 0
-    for j, kind, legs in calls[r]:
+    for j, kind, legs in calls.get(core, []):
         if j == r:
             g.wait_ge(S.qx, 1)
         else:
-            g.wait_ge(S[kind + str(slot[j])], arrive[(r, j, kind)][0])
-        view = codes(j).bitcast(dt.uint8) if kind == CODES else plane(j)
+            g.wait_ge(S[kind + str(slot[j])], adds[(core, j, kind)])
         transfers = []
         for d, eng in legs:
-            rid, pid = topo.addr(cores[d], core)
+            rid, pid = topo.addr(d, core)
             transfers.append(RemoteDMATransfer(dst_ids=[DstId(rid=rid, pnc=pid)], dma_engine_mask=sum(1 << e for e in eng),
-                                               remote_sem=S[kind + str(slot[j])], src=view, dst=view))
+                                               remote_sem=S[kind + str(slot[j])],
+                                               src=view(core, j, kind), dst=view(d, j, kind)))
             sent += len(eng)
         g.remote_dma_fused(transfers, local_sem=S.sent)
 
-    order = [r] + sorted((j for j in mem if j != r), key=lambda j: max(arrive[(r, j, k)][1] for k in (CODES, PLANE)))
+    if r is None:
+        g.wait_ge(S.sent, sent)
+        return
+
+    mem = [j for j in range(n) if seq[j] == seq[r]]
+    order = [r] + sorted((j for j in mem if j != r), key=lambda j: (j in late, wid[j]))
     g.tensor.wait_ge(S.qw, 1)
     g.tensor.wait_ge(S.qx, 1)
     for i, j in enumerate(order):
         if j != r:
-            for kind in (CODES, PLANE):
-                g.tensor.wait_ge(S[kind + str(slot[j])], arrive[(r, j, kind)][0])
+            for kind in (PLANE, CODES, REST) if j in cut else (PLANE, CODES):
+                g.tensor.wait_ge(S[kind + str(slot[j])], adds[(core, j, kind)])
         acc = T.ps[:, 512 * i:512 * i + wid[j]]
         blk = T.yb[:, out[j]:out[j] + wid[j]]
         done, copied = S["m" + str(i)], S["v" + str(i)]

@@ -13,12 +13,14 @@ SCRATCH = {
     "wp": ("sbuf", [128, 128], "uint8"),
     "xq": ("sbuf", [128, LAND], "float8_e4m3fn_x4"),
     "xp": ("sbuf", [128, LAND], "uint8"),
-    "xr": ("sbuf", [128, 128], "float8_e4m3fn_x4"),
-    "ps": ("psum", [128, 512 * MOST], "float32"),
+    "rq": ("sbuf", [128, LAND], "float8_e4m3fn_x4"),
+    "rp": ("sbuf", [128, LAND], "uint8"),
+    "ps": ("psum", [128, 512 * (MOST + 1)], "float32"),
     "yb": ("sbuf", [128, 808], "float32"),
 }
 SEMAPHORES = (["ldx", "ldw", "qx", "qw", "sent", "st"]
-              + [k + str(i) for k in ("c", "d", "p", "m", "v") for i in range(MOST)])
+              + [k + str(i) for k in ("c", "d", "p", "kc", "kd", "kp") for i in range(MOST)]
+              + [k + str(i) for k in ("m", "v") for i in range(MOST + 1)])
 
 CODES, REST, PLANE = "c", "d", "p"
 _KEEP = {}
@@ -47,10 +49,10 @@ def _plan(cores, seq, wid, topo):
     def home(c, d):
         return [e for e in full(c, d) if e not in away(c)]
 
-    calls, cut, late, park = {}, set(), set(), set()
+    calls, cut, late = {}, set(), set()
 
-    def call(c, j, kind, legs):
-        calls.setdefault(c, []).append((j, kind, legs))
+    def call(c, legs):
+        calls.setdefault(c, []).append(legs)
 
     for s in sorted(set(seq)):
         mem = [j for j in range(n) if seq[j] == s]
@@ -76,65 +78,73 @@ def _plan(cores, seq, wid, topo):
             for r in mem:
                 c = cores[r]
                 for j, kind, dsts in leave[r]:
-                    call(c, j, kind, [(cores[d], full(c, cores[d])[i::len(dsts)]) for i, d in enumerate(dsts)])
-                for j, kind, dsts in stay[r] + sorted(onward[r], key=lambda q: q[1] != CODES):
-                    call(c, j, kind, [(cores[d], home(c, cores[d])[i::len(dsts)]) for i, d in enumerate(dsts)])
+                    call(c, [(j, kind, cores[d], full(c, cores[d])[i::len(dsts)]) for i, d in enumerate(dsts)])
+                for j, kind, dsts in stay[r] + onward[r]:
+                    call(c, [(j, kind, cores[d], home(c, cores[d])[i::len(dsts)]) for i, d in enumerate(dsts)])
             continue
         mid = max((grp for grp in chips.values()
                    if all(topo.may_write(cores[a], cores[b]) and topo.may_write(cores[b], cores[a])
                           for a in grp for b in mem if a != b)), key=len)
         outer = [j for j in mem if j not in mid]
-        idle = sorted((c for c in range(WORLD) if place(c) == place(cores[mid[0]]) and c not in cores),
-                      key=lambda c: (topo.die(c) == topo.die(cores[mid[0]]), c))
-        carrier = {o: idle[i] for i, o in enumerate(outer)}
-        serves = {}
-        for o in outer:
-            for d in outer:
-                if d != o and not topo.may_write(cores[o], cores[d]):
-                    serves[d] = carrier[o]
-        for j in mid:
-            c = cores[j]
+        idle = [c for c in range(WORLD) if place(c) == place(cores[mid[0]]) and c not in cores
+                and topo.die(c) != topo.die(cores[mid[0]])]
+        porters = [idle[0], idle[-1]]
+        for k, j in enumerate(mid):
+            c, h = cores[j], porters[k % len(porters)]
             near = [d for d in mid if d != j]
-            round_ = [d for d in outer if d in serves and topo.same_plane(c, cores[d])]
-            straight = [d for d in outer if d not in round_]
-            call(c, j, CODES, [(cores[d], full(c, cores[d])[i::len(outer)]) for i, d in enumerate(outer)])
-            for d in round_:
-                call(c, j, PLANE, [(serves[d], home(c, serves[d]))])
-                call(serves[d], j, PLANE, [(cores[d], full(serves[d], cores[d]))])
-            if straight:
-                call(c, j, PLANE, [(cores[d], full(c, cores[d])[i::len(straight)]) for i, d in enumerate(straight)])
+            call(c, [(j, CODES, cores[d], full(c, cores[d])[i::len(outer)]) for i, d in enumerate(outer)])
+            call(c, [(j, PLANE, h, home(c, h))])
+            call(h, [(j, PLANE, cores[d], full(h, cores[d])[i::len(outer)]) for i, d in enumerate(outer)])
             for kind in (CODES, PLANE):
-                call(c, j, kind, [(cores[d], home(c, cores[d])[i::len(near)]) for i, d in enumerate(near)])
+                call(c, [(j, kind, cores[d], home(c, cores[d])[i::len(near)]) for i, d in enumerate(near)])
+        ma, mb = cores[mid[-1]], cores[mid[0]]
         for j in outer:
-            c, h = cores[j], carrier[j]
-            shut = [d for d in outer if d != j]
+            c = cores[j]
+            f = [cores[d] for d in outer if d != j and not topo.may_write(c, cores[d])][0]
+            ring = [b for b in cores if seq[cores.index(b)] != s and place(b) != place(c)
+                    and topo.may_write(c, b) and topo.may_write(b, f)]
+            beside = [b for b in cores if b != c and place(b) == place(c) and topo.may_write(b, mb)
+                      and topo.rack(topo.host(c)) != topo.rack(topo.host(mb))]
             late.add(j)
-            beside = [b for b in cores if b != c and place(b) == place(c) and topo.may_write(b, h)
-                      and topo.rack(topo.host(c)) != topo.rack(topo.host(h))]
             if wid[j] == 2 * PIECE and beside:
                 cut.add(j)
-                park.add((beside[0], j))
-                call(c, j, REST, [(beside[0], home(c, beside[0]))])
-                call(beside[0], j, REST, [(h, full(beside[0], h))])
-            for kind in (CODES, PLANE):
-                call(c, j, kind, [(h, full(c, h))])
-            for kind in (CODES, PLANE, REST) if j in cut else (CODES, PLANE):
-                call(h, j, kind, [(cores[d], full(h, cores[d])[i::len(shut)]) for i, d in enumerate(shut)]
-                     + [(cores[d], home(h, cores[d])[i::len(mid)]) for i, d in enumerate(mid)])
+                b = beside[0]
+                call(c, [(j, CODES, ma, full(c, ma)[0::2]), (j, REST, ring[1], full(c, ring[1])[1::2])])
+                call(c, [(j, REST, b, home(c, b))])
+                call(c, [(j, PLANE, ma, full(c, ma)[0::2]), (j, PLANE, ring[0], full(c, ring[0])[1::2])])
+                call(b, [(j, REST, mb, full(b, mb))])
+                call(mb, [(j, REST, ma, full(mb, ma))])
+                call(ma, [(j, CODES, f, full(ma, f)), (j, CODES, mb, home(ma, mb))])
+                call(ma, [(j, PLANE, mb, full(ma, mb))])
+                call(ring[1], [(j, REST, f, full(ring[1], f))])
+                call(ring[0], [(j, PLANE, f, full(ring[0], f))])
+            else:
+                for k, kind in enumerate((CODES, PLANE)):
+                    call(c, [(j, kind, ring[k], full(c, ring[k])[0::2]), (j, kind, ma, full(c, ma)[1::2])])
+                    call(ring[k], [(j, kind, f, full(ring[k], f))])
+                call(ma, [(j, CODES, mb, home(ma, mb))])
+                call(ma, [(j, PLANE, mb, full(ma, mb))])
+
+    def stage(c, legs):
+        j, kind = legs[0][0], legs[0][1]
+        if cores[j] == c:
+            return 0
+        return (4 if kind == PLANE else 2) + (j in cut)
 
     adds = {}
-    for c, todo in calls.items():
-        for j, kind, legs in todo:
-            for d, eng in legs:
+    for c in calls:
+        calls[c] = sorted(calls[c], key=lambda legs: stage(c, legs))
+        for legs in calls[c]:
+            for j, kind, d, eng in legs:
                 adds[(d, j, kind)] = len(eng)
-    return calls, adds, cut, late, park
+    return calls, adds, cut, late
 
 
 def rank_program(g, core, T, topo):
     cores, seq, wid, S = T.cores, T.tables["SEQ"], T.tables["WID"], T.sem
     if "plan" not in _KEEP:
         _KEEP["plan"] = _plan(cores, seq, wid, topo)
-    calls, adds, cut, late, park = _KEEP["plan"]
+    calls, adds, cut, late = _KEEP["plan"]
     r = T.rank_of(core)
     if r is None and core not in calls:
         return
@@ -152,15 +162,20 @@ def rank_program(g, core, T, topo):
     def plane(j):
         return T.xp[:, land[j]:land[j] + wid[j]]
 
+    def member(c, j):
+        return c in cores and seq[cores.index(c)] == seq[j]
+
+    def sem(c, j, kind):
+        return S[("" if member(c, j) else "k") + kind + str(slot[j])]
+
     def view(c, j, kind):
-        if kind == PLANE:
-            return plane(j)
-        if (c, j) in park:
-            return T.xr[:, :wid[j] - PIECE].bitcast(dt.uint8)
+        q, p = (T.xq, T.xp) if member(c, j) else (T.rq, T.rp)
         a, b = land[j], land[j] + wid[j]
+        if kind == PLANE:
+            return p[:, a:b]
         if j in cut:
             a, b = (a, a + PIECE) if kind == CODES else (a + PIECE, b)
-        return T.xq[:, a:b].bitcast(dt.uint8)
+        return q[:, a:b].bitcast(dt.uint8)
 
     if r is not None:
         g.sync.dma_start(T.xb[:, :4 * wid[r]], T.x[:, :4 * wid[r]]).then_inc(S.ldx, 16)
@@ -171,16 +186,17 @@ def rank_program(g, core, T, topo):
         g.vector.quantize_mx(T.wq[:], T.wp[:], T.wb[:]).then_inc(S.qw, 1)
 
     sent = 0
-    for j, kind, legs in calls.get(core, []):
-        if j == r:
-            g.wait_ge(S.qx, 1)
-        else:
-            g.wait_ge(S[kind + str(slot[j])], adds[(core, j, kind)])
+    for legs in calls.get(core, []):
+        for j, kind in sorted(set((leg[0], leg[1]) for leg in legs)):
+            if j == r:
+                g.wait_ge(S.qx, 1)
+            else:
+                g.wait_ge(sem(core, j, kind), adds[(core, j, kind)])
         transfers = []
-        for d, eng in legs:
+        for j, kind, d, eng in legs:
             rid, pid = topo.addr(d, core)
             transfers.append(RemoteDMATransfer(dst_ids=[DstId(rid=rid, pnc=pid)], dma_engine_mask=sum(1 << e for e in eng),
-                                               remote_sem=S[kind + str(slot[j])],
+                                               remote_sem=sem(d, j, kind),
                                                src=view(core, j, kind), dst=view(d, j, kind)))
             sent += len(eng)
         g.remote_dma_fused(transfers, local_sem=S.sent)
@@ -191,17 +207,25 @@ def rank_program(g, core, T, topo):
 
     mem = [j for j in range(n) if seq[j] == seq[r]]
     order = [r] + sorted((j for j in mem if j != r), key=lambda j: (j in late, wid[j]))
+    blocks = []
+    for j in order:
+        if j == r:
+            blocks.append((j, 0, wid[j], ()))
+        elif j in cut:
+            blocks += [(j, 0, PIECE, (PLANE, CODES)), (j, PIECE, wid[j], (REST,))]
+        else:
+            blocks.append((j, 0, wid[j], (PLANE, CODES)))
     g.tensor.wait_ge(S.qw, 1)
     g.tensor.wait_ge(S.qx, 1)
-    for i, j in enumerate(order):
-        if j != r:
-            for kind in (PLANE, CODES, REST) if j in cut else (PLANE, CODES):
-                g.tensor.wait_ge(S[kind + str(slot[j])], adds[(core, j, kind)])
-        acc = T.ps[:, 512 * i:512 * i + wid[j]]
-        blk = T.yb[:, out[j]:out[j] + wid[j]]
+    for i, (j, a, b, needs) in enumerate(blocks):
+        for kind in needs:
+            g.tensor.wait_ge(sem(core, j, kind), adds[(core, j, kind)])
+        acc = T.ps[:, 512 * i:512 * i + b - a]
+        blk = T.yb[:, out[j] + a:out[j] + b]
         done, copied = S["m" + str(i)], S["v" + str(i)]
-        g.tensor.matmul_mx(acc, T.wq[:], T.wp[:], codes(j), plane(j), True, True).then_inc(done, 1)
-        if (len(order) - 1 - i) % 2 == 0:
+        g.tensor.matmul_mx(acc, T.wq[:], T.wp[:], T.xq[:, land[j] + a:land[j] + b], T.xp[:, land[j] + a:land[j] + b],
+                           True, True).then_inc(done, 1)
+        if (len(blocks) - 1 - i) % 2 == 0:
             g.vector.wait_ge(done, 1)
             g.vector.tensor_copy(blk, acc).then_inc(copied, 1)
             q = g.sync
@@ -210,8 +234,8 @@ def rank_program(g, core, T, topo):
             g.scalar.activation(blk, acc, ActivationFunctionType.Copy).then_inc(copied, 1)
             q = g.scalar
         q.wait_ge(copied, 1)
-        q.dma_start(T.y[:, out[j]:out[j] + wid[j]], blk).then_inc(S.st, 16)
+        q.dma_start(T.y[:, out[j] + a:out[j] + b], blk).then_inc(S.st, 16)
 
     if sent:
         g.wait_ge(S.sent, sent)
-    g.wait_ge(S.st, 16 * len(order))
+    g.wait_ge(S.st, 16 * len(blocks))

from concourse.bass import DstId, RemoteDMATransfer
from concourse.mybir import dt, ActivationFunctionType

LAND = 832
MOST = 4
WORLD = 512
PIECE = 128

SCRATCH = {
    "xb": ("sbuf", [128, 1024], "bfloat16"),
    "wb": ("sbuf", [128, 512], "bfloat16"),
    "wq": ("sbuf", [128, 128], "float8_e4m3fn_x4"),
    "wp": ("sbuf", [128, 128], "uint8"),
    "xq": ("sbuf", [128, LAND], "float8_e4m3fn_x4"),
    "xp": ("sbuf", [128, LAND], "uint8"),
    "rq": ("sbuf", [128, LAND], "float8_e4m3fn_x4"),
    "rp": ("sbuf", [128, LAND], "uint8"),
    "ps": ("psum", [128, 512 * (MOST + 1)], "float32"),
    "yb": ("sbuf", [128, 808], "float32"),
}
SEMAPHORES = (["ldx", "ldw", "qx", "qw", "sent", "st"]
              + [k + str(i) for k in ("c", "d", "p", "kc", "kd", "kp") for i in range(MOST)]
              + [k + str(i) for k in ("m", "v") for i in range(MOST + 1)])

CODES, REST, PLANE = "c", "d", "p"
_KEEP = {}


def _engines(mask):
    return [e for e in range(mask.bit_length()) if (mask >> e) & 1]


def _plan(cores, seq, wid, topo):
    n = len(cores)

    def place(c):
        return (topo.host(c), topo.chip(c))

    def away(c):
        out = set()
        for d in cores:
            if place(d) != place(c) and topo.may_write(c, d):
                out |= set(_engines(topo.mask(c, d)))
        return out

    def full(c, d):
        return _engines(topo.mask(c, d))

    def home(c, d):
        return [e for e in full(c, d) if e not in away(c)]

    calls, cut, late = {}, set(), set()

    def call(c, legs):
        calls.setdefault(c, []).append(legs)

    for s in sorted(set(seq)):
        mem = [j for j in range(n) if seq[j] == s]
        chips = {}
        for j in mem:
            chips.setdefault(place(cores[j]), []).append(j)
        if all(topo.may_write(cores[a], cores[b]) for a in mem for b in mem if a != b):
            leave, stay, onward = {j: [] for j in mem}, {j: [] for j in mem}, {j: [] for j in mem}
            for j in mem:
                near = [d for d in chips[place(cores[j])] if d != j]
                reach = [grp for pl, grp in chips.items() if pl != place(cores[j])]
                for k, kind in enumerate((CODES, PLANE)):
                    gates = [grp[(mem.index(j) + k) % len(grp)] for grp in reach]
                    if gates:
                        leave[j].append((j, kind, gates))
                    if near:
                        stay[j].append((j, kind, near))
                    for grp, gate in zip(reach, gates):
                        more = [d for d in grp if d != gate]
                        if more:
                            onward[gate].append((j, kind, more))
                            late.add(j)
            for r in mem:
                c = cores[r]
                for j, kind, dsts in leave[r]:
                    call(c, [(j, kind, cores[d], full(c, cores[d])[i::len(dsts)]) for i, d in enumerate(dsts)])
                for j, kind, dsts in stay[r] + onward[r]:
                    call(c, [(j, kind, cores[d], home(c, cores[d])[i::len(dsts)]) for i, d in enumerate(dsts)])
            continue
        mid = max((grp for grp in chips.values()
                   if all(topo.may_write(cores[a], cores[b]) and topo.may_write(cores[b], cores[a])
                          for a in grp for b in mem if a != b)), key=len)
        outer = [j for j in mem if j not in mid]
        idle = [c for c in range(WORLD) if place(c) == place(cores[mid[0]]) and c not in cores
                and topo.die(c) != topo.die(cores[mid[0]])]
        porters = [idle[0], idle[-1]]
        for k, j in enumerate(mid):
            c, h = cores[j], porters[k % len(porters)]
            near = [d for d in mid if d != j]
            call(c, [(j, CODES, cores[d], full(c, cores[d])[i::len(outer)]) for i, d in enumerate(outer)])
            call(c, [(j, PLANE, h, home(c, h))])
            call(h, [(j, PLANE, cores[d], full(h, cores[d])[i::len(outer)]) for i, d in enumerate(outer)])
            for kind in (CODES, PLANE):
                call(c, [(j, kind, cores[d], home(c, cores[d])[i::len(near)]) for i, d in enumerate(near)])
        ma, mb = cores[mid[-1]], cores[mid[0]]
        for j in outer:
            c = cores[j]
            f = [cores[d] for d in outer if d != j and not topo.may_write(c, cores[d])][0]
            ring = [b for b in cores if seq[cores.index(b)] != s and place(b) != place(c)
                    and topo.may_write(c, b) and topo.may_write(b, f)]
            beside = [b for b in cores if b != c and place(b) == place(c) and topo.may_write(b, mb)
                      and topo.rack(topo.host(c)) != topo.rack(topo.host(mb))]
            late.add(j)
            if wid[j] == 2 * PIECE and beside:
                cut.add(j)
                b = beside[0]
                call(c, [(j, CODES, ma, full(c, ma)[0::2]), (j, REST, ring[1], full(c, ring[1])[1::2])])
                call(c, [(j, REST, b, home(c, b))])
                call(c, [(j, PLANE, ma, full(c, ma)[0::2]), (j, PLANE, ring[0], full(c, ring[0])[1::2])])
                call(b, [(j, REST, mb, full(b, mb))])
                call(mb, [(j, REST, ma, full(mb, ma))])
                call(ma, [(j, CODES, f, full(ma, f)), (j, CODES, mb, home(ma, mb))])
                call(ma, [(j, PLANE, mb, full(ma, mb))])
                call(ring[1], [(j, REST, f, full(ring[1], f))])
                call(ring[0], [(j, PLANE, f, full(ring[0], f))])
            else:
                for k, kind in enumerate((CODES, PLANE)):
                    call(c, [(j, kind, ring[k], full(c, ring[k])[0::2]), (j, kind, ma, full(c, ma)[1::2])])
                    call(ring[k], [(j, kind, f, full(ring[k], f))])
                call(ma, [(j, CODES, mb, home(ma, mb))])
                call(ma, [(j, PLANE, mb, full(ma, mb))])

    def stage(c, legs):
        j, kind = legs[0][0], legs[0][1]
        if cores[j] == c:
            return 0
        return (4 if kind == PLANE else 2) + (j in cut)

    adds = {}
    for c in calls:
        calls[c] = sorted(calls[c], key=lambda legs: stage(c, legs))
        for legs in calls[c]:
            for j, kind, d, eng in legs:
                adds[(d, j, kind)] = len(eng)
    return calls, adds, cut, late


def rank_program(g, core, T, topo):
    cores, seq, wid, S = T.cores, T.tables["SEQ"], T.tables["WID"], T.sem
    if "plan" not in _KEEP:
        _KEEP["plan"] = _plan(cores, seq, wid, topo)
    calls, adds, cut, late = _KEEP["plan"]
    r = T.rank_of(core)
    if r is None and core not in calls:
        return
    n = len(cores)
    slot, land, out = {}, {}, {}
    for s in set(seq):
        a = b = 0
        for i, j in enumerate(j for j in range(n) if seq[j] == s):
            slot[j], land[j], out[j] = i, a, b
            a, b = a + (wid[j] + 15) // 16 * 16, b + wid[j]

    def codes(j):
        return T.xq[:, land[j]:land[j] + wid[j]]

    def plane(j):
        return T.xp[:, land[j]:land[j] + wid[j]]

    def member(c, j):
        return c in cores and seq[cores.index(c)] == seq[j]

    def sem(c, j, kind):
        return S[("" if member(c, j) else "k") + kind + str(slot[j])]

    def view(c, j, kind):
        q, p = (T.xq, T.xp) if member(c, j) else (T.rq, T.rp)
        a, b = land[j], land[j] + wid[j]
        if kind == PLANE:
            return p[:, a:b]
        if j in cut:
            a, b = (a, a + PIECE) if kind == CODES else (a + PIECE, b)
        return q[:, a:b].bitcast(dt.uint8)

    if r is not None:
        g.sync.dma_start(T.xb[:, :4 * wid[r]], T.x[:, :4 * wid[r]]).then_inc(S.ldx, 16)
        g.sync.dma_start(T.wb[:], T.w[:]).then_inc(S.ldw, 16)
        g.vector.wait_ge(S.ldx, 16)
        g.vector.quantize_mx(codes(r), plane(r), T.xb[:, :4 * wid[r]]).then_inc(S.qx, 1)
        g.vector.wait_ge(S.ldw, 16)
        g.vector.quantize_mx(T.wq[:], T.wp[:], T.wb[:]).then_inc(S.qw, 1)

    sent = 0
    for legs in calls.get(core, []):
        for j, kind in sorted(set((leg[0], leg[1]) for leg in legs)):
            if j == r:
                g.wait_ge(S.qx, 1)
            else:
                g.wait_ge(sem(core, j, kind), adds[(core, j, kind)])
        transfers = []
        for j, kind, d, eng in legs:
            rid, pid = topo.addr(d, core)
            transfers.append(RemoteDMATransfer(dst_ids=[DstId(rid=rid, pnc=pid)], dma_engine_mask=sum(1 << e for e in eng),
                                               remote_sem=sem(d, j, kind),
                                               src=view(core, j, kind), dst=view(d, j, kind)))
            sent += len(eng)
        g.remote_dma_fused(transfers, local_sem=S.sent)

    if r is None:
        g.wait_ge(S.sent, sent)
        return

    mem = [j for j in range(n) if seq[j] == seq[r]]
    order = [r] + sorted((j for j in mem if j != r), key=lambda j: (j in late, wid[j]))
    blocks = []
    for j in order:
        if j == r:
            blocks.append((j, 0, wid[j], ()))
        elif j in cut:
            blocks += [(j, 0, PIECE, (PLANE, CODES)), (j, PIECE, wid[j], (REST,))]
        else:
            blocks.append((j, 0, wid[j], (PLANE, CODES)))
    g.tensor.wait_ge(S.qw, 1)
    g.tensor.wait_ge(S.qx, 1)
    for i, (j, a, b, needs) in enumerate(blocks):
        for kind in needs:
            g.tensor.wait_ge(sem(core, j, kind), adds[(core, j, kind)])
        acc = T.ps[:, 512 * i:512 * i + b - a]
        blk = T.yb[:, out[j] + a:out[j] + b]
        done, copied = S["m" + str(i)], S["v" + str(i)]
        g.tensor.matmul_mx(acc, T.wq[:], T.wp[:], T.xq[:, land[j] + a:land[j] + b], T.xp[:, land[j] + a:land[j] + b],
                           True, True).then_inc(done, 1)
        if (len(blocks) - 1 - i) % 2 == 0:
            g.vector.wait_ge(done, 1)
            g.vector.tensor_copy(blk, acc).then_inc(copied, 1)
            q = g.sync
        else:
            g.scalar.wait_ge(done, 1)
            g.scalar.activation(blk, acc, ActivationFunctionType.Copy).then_inc(copied, 1)
            q = g.scalar
        q.wait_ge(copied, 1)
        q.dma_start(T.y[:, out[j] + a:out[j] + b], blk).then_inc(S.st, 16)

    if sent:
        g.wait_ge(S.sent, sent)
    g.wait_ge(S.st, 16 * len(blocks))
